import numpy as np
import ml_dtypes


def mxq(x, axis, fmt="e4m3"):
    dtype, down = {"e4m3": (ml_dtypes.float8_e4m3fn, 7), "e5m2": (ml_dtypes.float8_e5m2, 14)}[fmt]
    v = np.moveaxis(np.asarray(x, np.float32).astype(ml_dtypes.bfloat16).astype(np.float64), axis, -1)
    blocks = v.reshape(v.shape[:-1] + (-1, 32))
    amax = np.abs(blocks).max(-1, keepdims=True)
    byte = np.maximum(np.where(amax > 0, np.frexp(amax)[1] - 1 + 127, 0) - down, 1)
    scale = np.exp2(byte - 127.0)
    codes = (blocks / scale).astype(np.float32).astype(dtype).astype(np.float64)
    return np.moveaxis((codes * scale).reshape(v.shape), -1, axis)


WIDE = False


def mx_kscale(k):
    if not WIDE:
        return np.ones(k)
    levels = np.array([10, -10, 5, -5, 0])
    if k % 512:
        return np.exp2(np.random.permutation(np.resize(levels, k // 32))).repeat(32)
    a = np.empty((k // 512, 16))
    for p in range(k // 512):
        a[p, :8] = np.random.permutation(np.resize(levels, 8))
        for g in range(8):
            far = levels[np.abs(levels - a[p, g]) >= 10]
            a[p, g + 8] = far[np.random.randint(len(far))]
    return np.exp2(a.ravel()).repeat(32)


def f64(x):
    return np.asarray(x).astype(np.float64)


def striped(idx):
    return np.tile(idx.reshape(-1, 16).T, (8, 1)).astype(np.uint16)


def unstriped(offs):
    return offs[:16].T.reshape(-1).astype(np.int64)


def striped8(idx):
    return np.concatenate([x.reshape(-1, 16).T for x in idx]).astype(np.uint16)


def runs(offs, k):
    lists = np.stack([offs[16 * r : 16 * r + 16].T.reshape(-1) for r in range(8)]).astype(np.int64)
    return lists[np.arange(k) % 512 // 64]


def pack_weight(w):
    k, n = w.shape
    w = f64(np.asarray(w, np.float32).astype(ml_dtypes.bfloat16)).reshape(k // 32, 32, n)
    amax = np.abs(w).max(1)
    byte = np.clip(np.where(amax > 0, np.frexp(amax)[1] - 1 + 127 - 7, 1), 1, 254)
    scaled = (w * np.exp2(127.0 - byte)[:, None, :]).reshape(k, n).astype(np.float32)
    words = np.ascontiguousarray(scaled.reshape(k // 512, 128, 4, n).transpose(0, 1, 3, 2)).astype(ml_dtypes.float8_e4m3fn).view(np.uint8)
    return words, np.ascontiguousarray(byte.astype(np.uint8).reshape(k // 512, 16, n))


def unpack_weight(words, scales):
    g, p, n, _ = words.shape
    vals = np.ascontiguousarray(words).view(ml_dtypes.float8_e4m3fn).astype(np.float64) * np.repeat(np.exp2(scales.astype(np.float64) - 127.0), 8, axis=1)[..., None]
    return vals.transpose(0, 1, 3, 2).reshape(g * 512, n)

def planes(y):
    n, m = y.shape
    v = y.astype(np.float32).astype(ml_dtypes.bfloat16).astype(np.float64).reshape(n // 32, 32, m)
    top = np.abs(v).max(1)
    byte = np.clip(np.where(top > 0, np.frexp(top)[1] - 1 + 127 - 7, 1), 1, 254)
    codes = (v * np.exp2(127.0 - byte)[:, None, :]).reshape(n, m).astype(np.float32).astype(ml_dtypes.float8_e4m3fn).view(np.uint8)
    words = codes.reshape(n // 512, 128, 4, m).transpose(0, 1, 3, 2)
    return np.ascontiguousarray(words), np.ascontiguousarray(byte.astype(np.uint8).reshape(n // 512, 16, m))


K, T, S, N, H = 512, 2048, 512, 512, 512


def setup_inputs():
    n = np.random.standard_normal
    s = mx_kscale(K)[:, None]
    u = mx_kscale(H)
    packed_xT = pack_weight(n((K, T)) * s)
    packed_w1 = pack_weight(n((K, H)) / np.sqrt(K) / s)
    packed_w2 = pack_weight(n((H, N)) / np.sqrt(2 * H) / u[:, None])
    packed_w3 = pack_weight(n((K, N)) / np.sqrt(2 * K) / s)
    return {
        "x_words": packed_xT[0],
        "x_scales": packed_xT[1],
        "w1_words": packed_w1[0],
        "w1_scales": packed_w1[1],
        "gn": (np.random.uniform(0.5, 1.5, (H, 1)) * u[:, None]).astype(np.float32),
        "w2_words": packed_w2[0],
        "w2_scales": packed_w2[1],
        "w3_words": packed_w3[0],
        "w3_scales": packed_w3[1],
        "offs": striped(np.random.permutation(T)[:S]),
        "n1": striped8(np.stack([np.random.permutation(S) for _ in range(8)])),
        "n2": striped8(np.stack([np.random.permutation(S) for _ in range(8)])),
        "n3": striped8(np.stack([np.random.permutation(S) for _ in range(8)])),
        "two": striped(np.random.permutation(T)[:S]),
        "n4": striped8(np.stack([np.random.permutation(S) for _ in range(8)])),
        "n5": striped8(np.stack([np.random.permutation(S) for _ in range(8)])),
    }


def reference(x_words, x_scales, w1_words, w1_scales, gn, w2_words, w2_scales, w3_words, w3_scales, offs, n1, n2, n3, two, n4, n5):
    xq = unpack_weight(x_words, x_scales)[:, unstriped(offs)]
    y = unpack_weight(w1_words, w1_scales).T @ xq
    z = f64(gn) * (np.maximum(y, y[np.arange(H)[:, None], runs(n1, H)]) - (np.maximum(y[np.arange(H)[:, None], runs(n2, H)], y[np.arange(H)[:, None], runs(n3, H)])))
    x_two = unpack_weight(x_words, x_scales)[:, unstriped(two)]
    h = unpack_weight(w2_words, w2_scales).T @ mxq(z, 0, "e4m3") + unpack_weight(w3_words, w3_scales).T @ x_two
    out_0 = np.minimum(np.maximum(h, h[np.arange(N)[:, None], runs(n4, N)]), h[np.arange(N)[:, None], runs(n5, N)])
    return (out_0,) + planes(out_0)

@@ -1,0 +1,218 @@
+from contextlib import ExitStack
+
+import concourse.mybir as mybir
+
+K, T, S, N, H = 512, 2048, 512, 512, 512
+FLOPS = 2 * S * (K * H + H * N + K * N)
+
+F32 = mybir.dt.float32
+BF16 = mybir.dt.bfloat16
+I32 = mybir.dt.int32
+U32 = mybir.dt.uint32
+U16 = mybir.dt.uint16
+U8 = mybir.dt.uint8
+FP8X4 = mybir.dt.float8_e4m3fn_x4
+ALU = mybir.AluOpType
+ACT = mybir.ActivationFunctionType
+
+P = 128
+PACK = 4
+QUADS = 4
+HALF = S // 2
+CHUNKS = ((0, 256), (256, 128), (384, 128))
+VECTOR_TILES_Y = 3
+VECTOR_TILES_H = 2
+
+
+def tile_picked_mixinmixminmx_none_po_kernel(
+    tc, x_words, x_scales, w1_words, w1_scales, gn, w2_words, w2_scales, w3_words, w3_scales,
+    offs, n1, n2, n3, two, n4, n5, out_0, out_1, out_2,
+):
+    nc = tc.nc
+
+    with ExitStack() as ctx:
+        keep = ctx.enter_context(tc.tile_pool(name="keep", bufs=1))
+        psum = ctx.enter_context(tc.psum_pool(name="psum", bufs=1))
+
+        def sbuf(shape, dtype, name):
+            return keep.tile(shape, dtype, name=name, align_bytes=64)
+
+        def load_list(src, name):
+            dst = keep.tile([P, S // 16], U16, name=name)
+            nc.sync.dma_start(dst[:], src)
+            return dst
+
+        def load_words(src, width, name):
+            dst = sbuf([P, width], U32, name)
+            nc.sync.dma_start(dst[:].bitcast(I32), src[0].rearrange("p n t -> p (n t)").bitcast(I32))
+            return dst
+
+        def load_scale_rows(queue, dst, first_row, src):
+            for q in range(QUADS):
+                row = 32 * q + first_row
+                queue.dma_start(dst[row : row + 4, :].bitcast(I32), src[0, 4 * q : 4 * q + 4, :].bitcast(I32))
+
+        def deal_words(src, name):
+            dst = sbuf([P, H], U32, name)
+            nc.vector.tensor_copy(
+                dst[:].bitcast(I32).rearrange("p (t c i) -> p c t i", t=PACK, i=4),
+                src[:].bitcast(I32).rearrange("p (c i t) -> p c t i", t=PACK, i=4),
+            )
+            return dst
+
+        def deal_scales(src, name):
+            dst = sbuf([P, H], U8, name)
+            nc.vector.tensor_copy(
+                dst[:].rearrange("p (t m) -> p m t", t=PACK),
+                src[:].rearrange("p (m t) -> p m t", t=PACK),
+            )
+            return dst
+
+        def entries(lst, first, count):
+            return lst[:, first // 16 : (first + count) // 16]
+
+        def look_up(on_vector, dst, window, lst, first, count):
+            picked = window[:].indirect(entries(lst, first, count))
+            if on_vector:
+                nc.vector.tensor_copy(dst, picked)
+            else:
+                nc.scalar.activation(dst, picked, ACT.Copy)
+
+        xs = sbuf([P, T], U8, "xs")
+        w1s_raw = sbuf([P, H], U8, "w1s_raw")
+        w23s_raw = sbuf([P, H], U8, "w23s_raw")
+        for plane in (xs, w1s_raw, w23s_raw):
+            nc.vector.memset(plane[:].bitcast(I32), 0)
+
+        offs_sb = load_list(offs, "offs_sb")
+        xw = load_words(x_words, T, "xw")
+        gain = sbuf([P, PACK], F32, "gain")
+        nc.scalar.dma_start(gain[:], gn.rearrange("(p t) o -> p (t o)", t=PACK))
+        load_scale_rows(nc.scalar, xs, 0, x_scales)
+        load_scale_rows(nc.scalar, w1s_raw, 0, w1_scales)
+        w1_raw = load_words(w1_words, H, "w1_raw")
+        two_sb = load_list(two, "two_sb")
+        n1_sb = load_list(n1, "n1_sb")
+        n2_sb = load_list(n2, "n2_sb")
+        n3_sb = load_list(n3, "n3_sb")
+        w3_raw = load_words(w3_words, N, "w3_raw")
+        w2_raw = load_words(w2_words, N, "w2_raw")
+        load_scale_rows(nc.sync, w23s_raw, 0, w2_scales)
+        load_scale_rows(nc.sync, w23s_raw, 4, w3_scales)
+        n4_sb = load_list(n4, "n4_sb")
+        n5_sb = load_list(n5, "n5_sb")
+
+        size = sbuf([P, PACK], F32, "size")
+        nc.scalar.activation(size[:], gain[:], ACT.Abs)
+        not_negative = sbuf([P, PACK], F32, "not_negative")
+        nc.vector.tensor_scalar(not_negative[:], gain[:], 0.0, None, ALU.is_ge)
+        sign = sbuf([P, PACK], BF16, "sign")
+        nc.vector.tensor_scalar(sign[:], not_negative[:], 2.0, -1.0, ALU.mult, ALU.add)
+
+        xq_s = sbuf([P, S], U8, "xq_s")
+        nc.vector.tensor_copy(xq_s[:], xs[:].indirect(offs_sb[:]))
+        w1s = deal_scales(w1s_raw, "w1s")
+        x2_s = sbuf([P, S], U8, "x2_s")
+        nc.vector.tensor_copy(x2_s[:], xs[:].indirect(two_sb[:]))
+
+        xq_w = [sbuf([P, HALF], U32, "xq_w%d" % u) for u in range(2)]
+        nc.vector.tensor_copy(xq_w[0][:], xw[:].indirect(entries(offs_sb, 0, HALF)))
+        w1 = deal_words(w1_raw, "w1")
+        nc.vector.tensor_copy(xq_w[1][:], xw[:].indirect(entries(offs_sb, HALF, HALF)))
+
+        y = [sbuf([P, S], F32, "y%d" % t) for t in range(PACK)]
+        for t in range(PACK):
+            rows = slice(P * t, P * (t + 1))
+            for u in range(2):
+                cols = slice(HALF * u, HALF * (u + 1))
+                acc = psum.tile([P, HALF], F32, name="acc", tag="bank%d_%d" % (t, u))
+                nc.tensor.matmul_mx(
+                    out=acc[:], lhsT=w1[:, rows].bitcast(FP8X4), lhsT_scale=w1s[:, rows],
+                    rhs=xq_w[u][:].bitcast(FP8X4), rhs_scale=xq_s[:, cols], start=True, stop=True,
+                )
+                nc.scalar.activation(y[t][:, cols], acc[:], ACT.Copy, scale=size[:, t : t + 1])
+
+        x2_w = sbuf([P, S], U32, "x2_w")
+        nc.vector.tensor_copy(x2_w[:], xw[:].indirect(two_sb[:]))
+        w3 = deal_words(w3_raw, "w3")
+        w2 = deal_words(w2_raw, "w2")
+        w23s = deal_scales(w23s_raw, "w23s")
+
+        h_acc = []
+        for c, (first, width) in enumerate(CHUNKS):
+            cols = slice(first, first + width)
+            g1 = sbuf([P, PACK, width], F32, "g1_%d" % c)
+            g2 = sbuf([P, PACK, width], F32, "g2_%d" % c)
+            g3 = sbuf([P, PACK, width], F32, "g3_%d" % c)
+            m1 = sbuf([P, PACK, width], F32, "m1_%d" % c)
+            m2 = sbuf([P, PACK, width], F32, "m2_%d" % c)
+            for t in range(PACK):
+                look_up(t < VECTOR_TILES_Y, g1[:, t, :], y[t], n1_sb, first, width)
+                look_up(False, g2[:, t, :], y[t], n2_sb, first, width)
+                look_up(False, g3[:, t, :], y[t], n3_sb, first, width)
+            for t in range(PACK):
+                nc.vector.tensor_tensor(m1[:, t, :], y[t][:, cols], g1[:, t, :], ALU.max)
+                nc.vector.tensor_tensor(m2[:, t, :], g2[:, t, :], g3[:, t, :], ALU.max)
+            unsigned = sbuf([P, width, PACK], BF16, "unsigned%d" % c)
+            nc.vector.tensor_tensor(
+                unsigned[:].rearrange("p (c i) t -> p c t i", i=4),
+                m1[:].rearrange("p t (c i) -> p c t i", i=4),
+                m2[:].rearrange("p t (c i) -> p c t i", i=4),
+                ALU.subtract,
+            )
+            z = sbuf([P, width, PACK], BF16, "z%d" % c)
+            nc.vector.tensor_tensor(
+                z[:], unsigned[:], sign[:].unsqueeze(1).to_broadcast([P, width, PACK]), ALU.mult
+            )
+            z_w = sbuf([P, width], U32, "z_w%d" % c)
+            z_s = sbuf([P, width], U8, "z_s%d" % c)
+            nc.vector.quantize_mx(out=z_w[:].bitcast(FP8X4), scales=z_s[:], in_=z[:].rearrange("p j t -> p (j t)"))
+            h_acc.append((z_w, z_s))
+
+        h = [sbuf([P, S], F32, "h%d" % t) for t in range(PACK)]
+        for c, (first, width) in enumerate(CHUNKS):
+            cols = slice(first, first + width)
+            z_w, z_s = h_acc[c]
+            for t in range(PACK):
+                rows = slice(P * t, P * (t + 1))
+                acc = psum.tile([P, width], F32, name="acc", tag="bank%d_%d" % (t, c % 2))
+                nc.tensor.matmul_mx(
+                    out=acc[:], lhsT=w3[:, rows].bitcast(FP8X4), lhsT_scale=w23s[4:P, rows],
+                    rhs=x2_w[:, cols].bitcast(FP8X4), rhs_scale=x2_s[:, cols], start=True, stop=False,
+                )
+                nc.tensor.matmul_mx(
+                    out=acc[:], lhsT=w2[:, rows].bitcast(FP8X4), lhsT_scale=w23s[:, rows],
+                    rhs=z_w[:].bitcast(FP8X4), rhs_scale=z_s[:], start=False, stop=True,
+                )
+                nc.scalar.activation(h[t][:, cols], acc[:], ACT.Copy)
+
+        out_rows = out_0.rearrange("(p t) j -> p t j", t=PACK)
+        out_words = out_1[0].rearrange("p n t -> p (n t)").bitcast(I32)
+        o_s = sbuf([P, S], U8, "o_s")
+        for c, (first, width) in enumerate(CHUNKS):
+            cols = slice(first, first + width)
+            g4 = sbuf([P, PACK, width], F32, "g4_%d" % c)
+            g5 = sbuf([P, PACK, width], F32, "g5_%d" % c)
+            m4 = sbuf([P, PACK, width], F32, "m4_%d" % c)
+            o = sbuf([P, PACK, width], F32, "o_%d" % c)
+            for t in range(PACK):
+                look_up(t < VECTOR_TILES_H, g4[:, t, :], h[t], n4_sb, first, width)
+                look_up(False, g5[:, t, :], h[t], n5_sb, first, width)
+            for t in range(PACK):
+                nc.vector.tensor_tensor(m4[:, t, :], h[t][:, cols], g4[:, t, :], ALU.max)
+            for t in range(PACK):
+                nc.vector.tensor_tensor(o[:, t, :], m4[:, t, :], g5[:, t, :], ALU.min)
+            nc.sync.dma_start(out_rows[:, :, cols], o[:])
+            rounded = sbuf([P, width, PACK], BF16, "rounded%d" % c)
+            nc.vector.tensor_copy(
+                rounded[:].rearrange("p (c i) t -> p c t i", i=4),
+                o[:].rearrange("p t (c i) -> p c t i", i=4),
+            )
+            o_w = sbuf([P, width], U32, "o_w%d" % c)
+            nc.vector.quantize_mx(
+                out=o_w[:].bitcast(FP8X4), scales=o_s[:, cols], in_=rounded[:].rearrange("p j t -> p (j t)")
+            )
+            nc.sync.dma_start(out_words[:, cols], o_w[:].bitcast(I32))
+        for q in range(QUADS):
+            queue = nc.sync if q % 2 == 0 else nc.scalar
+            queue.dma_start(out_2[0, 4 * q : 4 * q + 4, :].bitcast(I32), o_s[32 * q : 32 * q + 4, :].bitcast(I32))

@@ -20,8 +20,8 @@ PACK = 4
 QUADS = 4
 HALF = S // 2
 CHUNKS = ((0, 256), (256, 128), (384, 128))
-VECTOR_TILES_Y = 3
-VECTOR_TILES_H = 2
+VECTOR_TILES_Y = (4, 4, 2)
+VECTOR_TILES_H = (4, 1, 0)
 
 
 def tile_picked_mixinmixminmx_none_po_kernel(
@@ -42,13 +42,13 @@ def tile_picked_mixinmixminmx_none_po_kernel(
             nc.sync.dma_start(dst[:], src)
             return dst
 
-        def load_words(src, width, name):
-            dst = sbuf([P, width], U32, name)
+        def load_words(src, width, name, tag):
+            dst = keep.tile([P, width], U32, name=name, tag=tag, align_bytes=64)
             nc.sync.dma_start(dst[:].bitcast(I32), src[0].rearrange("p n t -> p (n t)").bitcast(I32))
             return dst
 
-        def load_scale_rows(queue, dst, first_row, src):
-            for q in range(QUADS):
+        def load_scale_rows(queues, dst, first_row, src):
+            for q, queue in enumerate(queues):
                 row = 32 * q + first_row
                 queue.dma_start(dst[row : row + 4, :].bitcast(I32), src[0, 4 * q : 4 * q + 4, :].bitcast(I32))
 
@@ -60,13 +60,11 @@ def tile_picked_mixinmixminmx_none_po_kernel(
             )
             return dst
 
-        def deal_scales(src, name):
-            dst = sbuf([P, H], U8, name)
+        def deal_scales(dst, src, first, last):
             nc.vector.tensor_copy(
-                dst[:].rearrange("p (t m) -> p m t", t=PACK),
-                src[:].rearrange("p (m t) -> p m t", t=PACK),
+                dst[:].rearrange("p (t m) -> p t m", t=PACK)[:, first:last, :],
+                src[:].rearrange("p (m t) -> p t m", t=PACK)[:, first:last, :],
             )
-            return dst
 
         def entries(lst, first, count):
             return lst[:, first // 16 : (first + count) // 16]
@@ -79,26 +77,28 @@ def tile_picked_mixinmixminmx_none_po_kernel(
                 nc.scalar.activation(dst, picked, ACT.Copy)
 
         xs = sbuf([P, T], U8, "xs")
-        w1s_raw = sbuf([P, H], U8, "w1s_raw")
+        w1s_raw = keep.tile([P, H], U8, name="w1s_raw", tag="w1s_raw", align_bytes=64)
         w23s_raw = sbuf([P, H], U8, "w23s_raw")
-        for plane in (xs, w1s_raw, w23s_raw):
-            nc.vector.memset(plane[:].bitcast(I32), 0)
+        nc.vector.memset(xs[:, : T // 2].bitcast(I32), 0)
+        nc.gpsimd.memset(xs[:, T // 2 :].bitcast(I32), 0)
+        nc.vector.memset(w1s_raw[:].bitcast(I32), 0)
+        nc.gpsimd.memset(w23s_raw[:].bitcast(I32), 0)
 
         offs_sb = load_list(offs, "offs_sb")
-        xw = load_words(x_words, T, "xw")
+        two_sb = load_list(two, "two_sb")
         gain = sbuf([P, PACK], F32, "gain")
         nc.scalar.dma_start(gain[:], gn.rearrange("(p t) o -> p (t o)", t=PACK))
-        load_scale_rows(nc.scalar, xs, 0, x_scales)
-        load_scale_rows(nc.scalar, w1s_raw, 0, w1_scales)
-        w1_raw = load_words(w1_words, H, "w1_raw")
-        two_sb = load_list(two, "two_sb")
+        load_scale_rows([nc.sync, nc.sync, nc.scalar, nc.scalar], xs, 0, x_scales)
+        xw = load_words(x_words, T, "xw", "xw")
+        w1_raw = load_words(w1_words, H, "w1_raw", "w1_raw")
+        load_scale_rows([nc.sync] * QUADS, w1s_raw, 0, w1_scales)
         n1_sb = load_list(n1, "n1_sb")
         n2_sb = load_list(n2, "n2_sb")
         n3_sb = load_list(n3, "n3_sb")
-        w3_raw = load_words(w3_words, N, "w3_raw")
-        w2_raw = load_words(w2_words, N, "w2_raw")
-        load_scale_rows(nc.sync, w23s_raw, 0, w2_scales)
-        load_scale_rows(nc.sync, w23s_raw, 4, w3_scales)
+        w3_raw = load_words(w3_words, N, "w3_raw", "w3_raw")
+        w2_raw = load_words(w2_words, N, "w2_raw", "w2_raw")
+        load_scale_rows([nc.sync] * QUADS, w23s_raw, 0, w2_scales)
+        load_scale_rows([nc.sync] * QUADS, w23s_raw, 4, w3_scales)
         n4_sb = load_list(n4, "n4_sb")
         n5_sb = load_list(n5, "n5_sb")
 
@@ -111,14 +111,16 @@ def tile_picked_mixinmixminmx_none_po_kernel(
 
         xq_s = sbuf([P, S], U8, "xq_s")
         nc.vector.tensor_copy(xq_s[:], xs[:].indirect(offs_sb[:]))
-        w1s = deal_scales(w1s_raw, "w1s")
         x2_s = sbuf([P, S], U8, "x2_s")
         nc.vector.tensor_copy(x2_s[:], xs[:].indirect(two_sb[:]))
 
         xq_w = [sbuf([P, HALF], U32, "xq_w%d" % u) for u in range(2)]
         nc.vector.tensor_copy(xq_w[0][:], xw[:].indirect(entries(offs_sb, 0, HALF)))
-        w1 = deal_words(w1_raw, "w1")
         nc.vector.tensor_copy(xq_w[1][:], xw[:].indirect(entries(offs_sb, HALF, HALF)))
+        w1 = deal_words(w1_raw, "w1")
+        w1s = sbuf([P, H], U8, "w1s")
+        deal_scales(w1s, w1s_raw, 0, 1)
+        deal_scales(w1s, w1s_raw, 1, PACK)
 
         y = [sbuf([P, S], F32, "y%d" % t) for t in range(PACK)]
         for t in range(PACK):
@@ -132,11 +134,12 @@ def tile_picked_mixinmixminmx_none_po_kernel(
                 )
                 nc.scalar.activation(y[t][:, cols], acc[:], ACT.Copy, scale=size[:, t : t + 1])
 
-        x2_w = sbuf([P, S], U32, "x2_w")
+        x2_w = keep.tile([P, S], U32, name="x2_w", tag="w1s_raw", align_bytes=64)
         nc.vector.tensor_copy(x2_w[:], xw[:].indirect(two_sb[:]))
         w3 = deal_words(w3_raw, "w3")
         w2 = deal_words(w2_raw, "w2")
-        w23s = deal_scales(w23s_raw, "w23s")
+        w23s = sbuf([P, N], U8, "w23s")
+        deal_scales(w23s, w23s_raw, 0, PACK)
 
         h_acc = []
         for c, (first, width) in enumerate(CHUNKS):
@@ -147,7 +150,7 @@ def tile_picked_mixinmixminmx_none_po_kernel(
             m1 = sbuf([P, PACK, width], F32, "m1_%d" % c)
             m2 = sbuf([P, PACK, width], F32, "m2_%d" % c)
             for t in range(PACK):
-                look_up(t < VECTOR_TILES_Y, g1[:, t, :], y[t], n1_sb, first, width)
+                look_up(t < VECTOR_TILES_Y[c], g1[:, t, :], y[t], n1_sb, first, width)
                 look_up(False, g2[:, t, :], y[t], n2_sb, first, width)
                 look_up(False, g3[:, t, :], y[t], n3_sb, first, width)
             for t in range(PACK):
@@ -184,7 +187,10 @@ def tile_picked_mixinmixminmx_none_po_kernel(
                     out=acc[:], lhsT=w2[:, rows].bitcast(FP8X4), lhsT_scale=w23s[:, rows],
                     rhs=z_w[:].bitcast(FP8X4), rhs_scale=z_s[:], start=False, stop=True,
                 )
-                nc.scalar.activation(h[t][:, cols], acc[:], ACT.Copy)
+                if c == len(CHUNKS) - 1 and t % 2 == 1:
+                    nc.vector.tensor_copy(h[t][:, cols], acc[:])
+                else:
+                    nc.scalar.activation(h[t][:, cols], acc[:], ACT.Copy)
 
         out_rows = out_0.rearrange("(p t) j -> p t j", t=PACK)
         out_words = out_1[0].rearrange("p n t -> p (n t)").bitcast(I32)
@@ -196,7 +202,7 @@ def tile_picked_mixinmixminmx_none_po_kernel(
             m4 = sbuf([P, PACK, width], F32, "m4_%d" % c)
             o = sbuf([P, PACK, width], F32, "o_%d" % c)
             for t in range(PACK):
-                look_up(t < VECTOR_TILES_H, g4[:, t, :], h[t], n4_sb, first, width)
+                look_up(t < VECTOR_TILES_H[c], g4[:, t, :], h[t], n4_sb, first, width)
                 look_up(False, g5[:, t, :], h[t], n5_sb, first, width)
             for t in range(PACK):
                 nc.vector.tensor_tensor(m4[:, t, :], h[t][:, cols], g4[:, t, :], ALU.max)

@@ -20,7 +20,6 @@ PACK = 4
 QUADS = 4
 HALF = S // 2
 CHUNKS = ((0, 256), (256, 128), (384, 128))
-VECTOR_TILES_Y = (4, 4, 2)
 VECTOR_TILES_H = (4, 1, 0)
 
 
@@ -52,19 +51,26 @@ def tile_picked_mixinmixminmx_none_po_kernel(
                 row = 32 * q + first_row
                 queue.dma_start(dst[row : row + 4, :].bitcast(I32), src[0, 4 * q : 4 * q + 4, :].bitcast(I32))
 
-        def deal_words(src, name):
+        def deal_words(engine, src, name):
             dst = sbuf([P, H], U32, name)
-            nc.vector.tensor_copy(
+            engine.tensor_copy(
                 dst[:].bitcast(I32).rearrange("p (t c i) -> p c t i", t=PACK, i=4),
                 src[:].bitcast(I32).rearrange("p (c i t) -> p c t i", t=PACK, i=4),
             )
             return dst
 
-        def deal_scales(dst, src, first, last):
-            nc.vector.tensor_copy(
-                dst[:].rearrange("p (t m) -> p t m", t=PACK)[:, first:last, :],
-                src[:].rearrange("p (m t) -> p t m", t=PACK)[:, first:last, :],
+        def deal_scales(src, name):
+            dst = sbuf([P, H], U8, name)
+            nc.gpsimd.tensor_copy(
+                dst[:].rearrange("p (t m) -> p t m", t=PACK),
+                src[:].rearrange("p (m t) -> p t m", t=PACK),
             )
+            return dst
+
+        def pieces(c):
+            width = CHUNKS[c][1]
+            step = width // 2 if c == len(CHUNKS) - 1 else width
+            return [slice(a, a + step) for a in range(0, width, step)]
 
         def entries(lst, first, count):
             return lst[:, first // 16 : (first + count) // 16]
@@ -77,7 +83,7 @@ def tile_picked_mixinmixminmx_none_po_kernel(
                 nc.scalar.activation(dst, picked, ACT.Copy)
 
         xs = sbuf([P, T], U8, "xs")
-        w1s_raw = keep.tile([P, H], U8, name="w1s_raw", tag="w1s_raw", align_bytes=64)
+        w1s_raw = sbuf([P, H], U8, "w1s_raw")
         w23s_raw = sbuf([P, H], U8, "w23s_raw")
         nc.vector.memset(xs[:, : T // 2].bitcast(I32), 0)
         nc.gpsimd.memset(xs[:, T // 2 :].bitcast(I32), 0)
@@ -90,8 +96,8 @@ def tile_picked_mixinmixminmx_none_po_kernel(
         nc.scalar.dma_start(gain[:], gn.rearrange("(p t) o -> p (t o)", t=PACK))
         load_scale_rows([nc.sync, nc.sync, nc.scalar, nc.scalar], xs, 0, x_scales)
         xw = load_words(x_words, T, "xw", "xw")
-        w1_raw = load_words(w1_words, H, "w1_raw", "w1_raw")
         load_scale_rows([nc.sync] * QUADS, w1s_raw, 0, w1_scales)
+        w1_raw = load_words(w1_words, H, "w1_raw", "w1_raw")
         n1_sb = load_list(n1, "n1_sb")
         n2_sb = load_list(n2, "n2_sb")
         n3_sb = load_list(n3, "n3_sb")
@@ -117,10 +123,8 @@ def tile_picked_mixinmixminmx_none_po_kernel(
         xq_w = [sbuf([P, HALF], U32, "xq_w%d" % u) for u in range(2)]
         nc.vector.tensor_copy(xq_w[0][:], xw[:].indirect(entries(offs_sb, 0, HALF)))
         nc.vector.tensor_copy(xq_w[1][:], xw[:].indirect(entries(offs_sb, HALF, HALF)))
-        w1 = deal_words(w1_raw, "w1")
-        w1s = sbuf([P, H], U8, "w1s")
-        deal_scales(w1s, w1s_raw, 0, 1)
-        deal_scales(w1s, w1s_raw, 1, PACK)
+        w1 = deal_words(nc.vector, w1_raw, "w1")
+        w1s = deal_scales(w1s_raw, "w1s")
 
         y = [sbuf([P, S], F32, "y%d" % t) for t in range(PACK)]
         for t in range(PACK):
@@ -134,12 +138,11 @@ def tile_picked_mixinmixminmx_none_po_kernel(
                 )
                 nc.scalar.activation(y[t][:, cols], acc[:], ACT.Copy, scale=size[:, t : t + 1])
 
-        x2_w = keep.tile([P, S], U32, name="x2_w", tag="w1s_raw", align_bytes=64)
+        x2_w = keep.tile([P, S], U32, name="x2_w", tag="w1_raw", align_bytes=64)
         nc.vector.tensor_copy(x2_w[:], xw[:].indirect(two_sb[:]))
-        w3 = deal_words(w3_raw, "w3")
-        w2 = deal_words(w2_raw, "w2")
-        w23s = sbuf([P, N], U8, "w23s")
-        deal_scales(w23s, w23s_raw, 0, PACK)
+        w3 = deal_words(nc.gpsimd, w3_raw, "w3")
+        w2 = deal_words(nc.gpsimd, w2_raw, "w2")
+        w23s = deal_scales(w23s_raw, "w23s")
 
         h_acc = []
         for c, (first, width) in enumerate(CHUNKS):
@@ -150,26 +153,31 @@ def tile_picked_mixinmixminmx_none_po_kernel(
             m1 = sbuf([P, PACK, width], F32, "m1_%d" % c)
             m2 = sbuf([P, PACK, width], F32, "m2_%d" % c)
             for t in range(PACK):
-                look_up(t < VECTOR_TILES_Y[c], g1[:, t, :], y[t], n1_sb, first, width)
+                look_up(True, g1[:, t, :], y[t], n1_sb, first, width)
                 look_up(False, g2[:, t, :], y[t], n2_sb, first, width)
                 look_up(False, g3[:, t, :], y[t], n3_sb, first, width)
             for t in range(PACK):
                 nc.vector.tensor_tensor(m1[:, t, :], y[t][:, cols], g1[:, t, :], ALU.max)
                 nc.vector.tensor_tensor(m2[:, t, :], g2[:, t, :], g3[:, t, :], ALU.max)
             unsigned = sbuf([P, width, PACK], BF16, "unsigned%d" % c)
-            nc.vector.tensor_tensor(
-                unsigned[:].rearrange("p (c i) t -> p c t i", i=4),
-                m1[:].rearrange("p t (c i) -> p c t i", i=4),
-                m2[:].rearrange("p t (c i) -> p c t i", i=4),
-                ALU.subtract,
-            )
             z = sbuf([P, width, PACK], BF16, "z%d" % c)
-            nc.vector.tensor_tensor(
-                z[:], unsigned[:], sign[:].unsqueeze(1).to_broadcast([P, width, PACK]), ALU.mult
-            )
             z_w = sbuf([P, width], U32, "z_w%d" % c)
             z_s = sbuf([P, width], U8, "z_s%d" % c)
-            nc.vector.quantize_mx(out=z_w[:].bitcast(FP8X4), scales=z_s[:], in_=z[:].rearrange("p j t -> p (j t)"))
+            for part in pieces(c):
+                nc.vector.tensor_tensor(
+                    unsigned[:, part, :].rearrange("p (c i) t -> p c t i", i=4),
+                    m1[:, :, part].rearrange("p t (c i) -> p c t i", i=4),
+                    m2[:, :, part].rearrange("p t (c i) -> p c t i", i=4),
+                    ALU.subtract,
+                )
+            for part in pieces(c):
+                signs = sign[:].unsqueeze(1).to_broadcast([P, part.stop - part.start, PACK])
+                nc.vector.tensor_tensor(z[:, part, :], unsigned[:, part, :], signs, ALU.mult)
+            for part in pieces(c):
+                nc.vector.quantize_mx(
+                    out=z_w[:, part].bitcast(FP8X4), scales=z_s[:, part],
+                    in_=z[:, part, :].rearrange("p j t -> p (j t)"),
+                )
             h_acc.append((z_w, z_s))
 
         h = [sbuf([P, S], F32, "h%d" % t) for t in range(PACK)]
@@ -210,14 +218,17 @@ def tile_picked_mixinmixminmx_none_po_kernel(
                 nc.vector.tensor_tensor(o[:, t, :], m4[:, t, :], g5[:, t, :], ALU.min)
             nc.sync.dma_start(out_rows[:, :, cols], o[:])
             rounded = sbuf([P, width, PACK], BF16, "rounded%d" % c)
-            nc.vector.tensor_copy(
-                rounded[:].rearrange("p (c i) t -> p c t i", i=4),
-                o[:].rearrange("p t (c i) -> p c t i", i=4),
-            )
             o_w = sbuf([P, width], U32, "o_w%d" % c)
-            nc.vector.quantize_mx(
-                out=o_w[:].bitcast(FP8X4), scales=o_s[:, cols], in_=rounded[:].rearrange("p j t -> p (j t)")
-            )
+            for part in pieces(c):
+                nc.vector.tensor_copy(
+                    rounded[:, part, :].rearrange("p (c i) t -> p c t i", i=4),
+                    o[:, :, part].rearrange("p t (c i) -> p c t i", i=4),
+                )
+            for part in pieces(c):
+                nc.vector.quantize_mx(
+                    out=o_w[:, part].bitcast(FP8X4), scales=o_s[:, first + part.start : first + part.stop],
+                    in_=rounded[:, part, :].rearrange("p j t -> p (j t)"),
+                )
             nc.sync.dma_start(out_words[:, cols], o_w[:].bitcast(I32))
         for q in range(QUADS):
             queue = nc.sync if q % 2 == 0 else nc.scalar

@@ -18,9 +18,14 @@ ACT = mybir.ActivationFunctionType
 P = 128
 PACK = 4
 QUADS = 4
+ROWS = 4
+GROUP = 16
+NEAR = 4
 HALF = S // 2
+
 CHUNKS = ((0, 256), (256, 128), (384, 128))
-VECTOR_TILES_H = (4, 1, 0)
+LAST = len(CHUNKS) - 1
+N4_ON_VECTOR = (4, 1, 0)
 
 
 def tile_picked_mixinmixminmx_none_po_kernel(
@@ -33,29 +38,32 @@ def tile_picked_mixinmixminmx_none_po_kernel(
         keep = ctx.enter_context(tc.tile_pool(name="keep", bufs=1))
         psum = ctx.enter_context(tc.psum_pool(name="psum", bufs=1))
 
-        def sbuf(shape, dtype, name):
-            return keep.tile(shape, dtype, name=name, align_bytes=64)
+        def sbuf(shape, dtype, name, tag=None):
+            return keep.tile(shape, dtype, name=name, tag=tag or name, align_bytes=64)
 
         def load_list(src, name):
-            dst = keep.tile([P, S // 16], U16, name=name)
+            dst = keep.tile([P, S // GROUP], U16, name=name)
             nc.sync.dma_start(dst[:], src)
             return dst
 
-        def load_words(src, width, name, tag):
-            dst = keep.tile([P, width], U32, name=name, tag=tag, align_bytes=64)
+        def load_words(src, width, name):
+            dst = sbuf([P, width], U32, name)
             nc.sync.dma_start(dst[:].bitcast(I32), src[0].rearrange("p n t -> p (n t)").bitcast(I32))
             return dst
 
         def load_scale_rows(queues, dst, first_row, src):
             for q, queue in enumerate(queues):
                 row = 32 * q + first_row
-                queue.dma_start(dst[row : row + 4, :].bitcast(I32), src[0, 4 * q : 4 * q + 4, :].bitcast(I32))
+                queue.dma_start(
+                    dst[row : row + ROWS, :].bitcast(I32),
+                    src[0, ROWS * q : ROWS * (q + 1), :].bitcast(I32),
+                )
 
         def deal_words(engine, src, name):
             dst = sbuf([P, H], U32, name)
             engine.tensor_copy(
-                dst[:].bitcast(I32).rearrange("p (t c i) -> p c t i", t=PACK, i=4),
-                src[:].bitcast(I32).rearrange("p (c i t) -> p c t i", t=PACK, i=4),
+                dst[:].bitcast(I32).rearrange("p (t c i) -> p c t i", t=PACK, i=NEAR),
+                src[:].bitcast(I32).rearrange("p (c i t) -> p c t i", t=PACK, i=NEAR),
             )
             return dst
 
@@ -69,11 +77,11 @@ def tile_picked_mixinmixminmx_none_po_kernel(
 
         def pieces(c):
             width = CHUNKS[c][1]
-            step = width // 2 if c == len(CHUNKS) - 1 else width
+            step = width // 2 if c == LAST else width
             return [slice(a, a + step) for a in range(0, width, step)]
 
         def entries(lst, first, count):
-            return lst[:, first // 16 : (first + count) // 16]
+            return lst[:, first // GROUP : (first + count) // GROUP]
 
         def look_up(on_vector, dst, window, lst, first, count):
             picked = window[:].indirect(entries(lst, first, count))
@@ -82,11 +90,17 @@ def tile_picked_mixinmixminmx_none_po_kernel(
             else:
                 nc.scalar.activation(dst, picked, ACT.Copy)
 
-        xs = sbuf([P, T], U8, "xs")
+        def by_tile(planes):
+            return planes.rearrange("p t (c i) -> p c t i", i=NEAR)
+
+        def side_by_side(grouped):
+            return grouped.rearrange("p (c i) t -> p c t i", i=NEAR)
+
+        x_s = sbuf([P, T], U8, "x_s")
         w1s_raw = sbuf([P, H], U8, "w1s_raw")
         w23s_raw = sbuf([P, H], U8, "w23s_raw")
-        nc.vector.memset(xs[:, : T // 2].bitcast(I32), 0)
-        nc.gpsimd.memset(xs[:, T // 2 :].bitcast(I32), 0)
+        nc.vector.memset(x_s[:, : T // 2].bitcast(I32), 0)
+        nc.gpsimd.memset(x_s[:, T // 2 :].bitcast(I32), 0)
         nc.vector.memset(w1s_raw[:].bitcast(I32), 0)
         nc.gpsimd.memset(w23s_raw[:].bitcast(I32), 0)
 
@@ -94,35 +108,33 @@ def tile_picked_mixinmixminmx_none_po_kernel(
         two_sb = load_list(two, "two_sb")
         gain = sbuf([P, PACK], F32, "gain")
         nc.scalar.dma_start(gain[:], gn.rearrange("(p t) o -> p (t o)", t=PACK))
-        load_scale_rows([nc.sync, nc.sync, nc.scalar, nc.scalar], xs, 0, x_scales)
-        xw = load_words(x_words, T, "xw", "xw")
+        load_scale_rows([nc.sync, nc.sync, nc.scalar, nc.scalar], x_s, 0, x_scales)
+        x_w = load_words(x_words, T, "x_w")
         load_scale_rows([nc.sync] * QUADS, w1s_raw, 0, w1_scales)
-        w1_raw = load_words(w1_words, H, "w1_raw", "w1_raw")
+        w1_raw = load_words(w1_words, H, "w1_raw")
         n1_sb = load_list(n1, "n1_sb")
         n2_sb = load_list(n2, "n2_sb")
         n3_sb = load_list(n3, "n3_sb")
-        w3_raw = load_words(w3_words, N, "w3_raw", "w3_raw")
-        w2_raw = load_words(w2_words, N, "w2_raw", "w2_raw")
+        w3_raw = load_words(w3_words, N, "w3_raw")
+        w2_raw = load_words(w2_words, N, "w2_raw")
         load_scale_rows([nc.sync] * QUADS, w23s_raw, 0, w2_scales)
-        load_scale_rows([nc.sync] * QUADS, w23s_raw, 4, w3_scales)
+        load_scale_rows([nc.sync] * QUADS, w23s_raw, ROWS, w3_scales)
         n4_sb = load_list(n4, "n4_sb")
         n5_sb = load_list(n5, "n5_sb")
 
         size = sbuf([P, PACK], F32, "size")
         nc.scalar.activation(size[:], gain[:], ACT.Abs)
-        not_negative = sbuf([P, PACK], F32, "not_negative")
-        nc.vector.tensor_scalar(not_negative[:], gain[:], 0.0, None, ALU.is_ge)
         sign = sbuf([P, PACK], BF16, "sign")
-        nc.vector.tensor_scalar(sign[:], not_negative[:], 2.0, -1.0, ALU.mult, ALU.add)
+        nc.scalar.activation(sign[:], gain[:], ACT.Sign)
 
         xq_s = sbuf([P, S], U8, "xq_s")
-        nc.vector.tensor_copy(xq_s[:], xs[:].indirect(offs_sb[:]))
-        x2_s = sbuf([P, S], U8, "x2_s")
-        nc.vector.tensor_copy(x2_s[:], xs[:].indirect(two_sb[:]))
+        nc.vector.tensor_copy(xq_s[:], x_s[:].indirect(offs_sb[:]))
+        x2_s = [sbuf([P, HALF], U8, "x2_s0")]
+        nc.vector.tensor_copy(x2_s[0][:], x_s[:].indirect(entries(two_sb, 0, HALF)))
 
         xq_w = [sbuf([P, HALF], U32, "xq_w%d" % u) for u in range(2)]
-        nc.vector.tensor_copy(xq_w[0][:], xw[:].indirect(entries(offs_sb, 0, HALF)))
-        nc.vector.tensor_copy(xq_w[1][:], xw[:].indirect(entries(offs_sb, HALF, HALF)))
+        for u in range(2):
+            nc.vector.tensor_copy(xq_w[u][:], x_w[:].indirect(entries(offs_sb, HALF * u, HALF)))
         w1 = deal_words(nc.vector, w1_raw, "w1")
         w1s = deal_scales(w1s_raw, "w1s")
 
@@ -138,13 +150,15 @@ def tile_picked_mixinmixminmx_none_po_kernel(
                 )
                 nc.scalar.activation(y[t][:, cols], acc[:], ACT.Copy, scale=size[:, t : t + 1])
 
-        x2_w = keep.tile([P, S], U32, name="x2_w", tag="w1_raw", align_bytes=64)
-        nc.vector.tensor_copy(x2_w[:], xw[:].indirect(two_sb[:]))
+        x2_s.append(sbuf([P, HALF], U8, "x2_s1", tag="w1s_raw"))
+        nc.vector.tensor_copy(x2_s[1][:], x_s[:].indirect(entries(two_sb, HALF, HALF)))
+        x2_w = sbuf([P, S], U32, "x2_w", tag="w1_raw")
+        nc.vector.tensor_copy(x2_w[:], x_w[:].indirect(two_sb[:]))
         w3 = deal_words(nc.gpsimd, w3_raw, "w3")
         w2 = deal_words(nc.gpsimd, w2_raw, "w2")
         w23s = deal_scales(w23s_raw, "w23s")
 
-        h_acc = []
+        z_mx = []
         for c, (first, width) in enumerate(CHUNKS):
             cols = slice(first, first + width)
             g1 = sbuf([P, PACK, width], F32, "g1_%d" % c)
@@ -165,9 +179,7 @@ def tile_picked_mixinmixminmx_none_po_kernel(
             z_s = sbuf([P, width], U8, "z_s%d" % c)
             for part in pieces(c):
                 nc.vector.tensor_tensor(
-                    unsigned[:, part, :].rearrange("p (c i) t -> p c t i", i=4),
-                    m1[:, :, part].rearrange("p t (c i) -> p c t i", i=4),
-                    m2[:, :, part].rearrange("p t (c i) -> p c t i", i=4),
+                    side_by_side(unsigned[:, part, :]), by_tile(m1[:, :, part]), by_tile(m2[:, :, part]),
                     ALU.subtract,
                 )
             for part in pieces(c):
@@ -178,58 +190,61 @@ def tile_picked_mixinmixminmx_none_po_kernel(
                     out=z_w[:, part].bitcast(FP8X4), scales=z_s[:, part],
                     in_=z[:, part, :].rearrange("p j t -> p (j t)"),
                 )
-            h_acc.append((z_w, z_s))
+            z_mx.append((z_w, z_s))
 
         h = [sbuf([P, S], F32, "h%d" % t) for t in range(PACK)]
         for c, (first, width) in enumerate(CHUNKS):
             cols = slice(first, first + width)
-            z_w, z_s = h_acc[c]
+            z_w, z_s = z_mx[c]
+            x2_scale = x2_s[first // HALF][:, first % HALF : first % HALF + width]
             for t in range(PACK):
                 rows = slice(P * t, P * (t + 1))
                 acc = psum.tile([P, width], F32, name="acc", tag="bank%d_%d" % (t, c % 2))
                 nc.tensor.matmul_mx(
-                    out=acc[:], lhsT=w3[:, rows].bitcast(FP8X4), lhsT_scale=w23s[4:P, rows],
-                    rhs=x2_w[:, cols].bitcast(FP8X4), rhs_scale=x2_s[:, cols], start=True, stop=False,
+                    out=acc[:], lhsT=w3[:, rows].bitcast(FP8X4), lhsT_scale=w23s[ROWS:P, rows],
+                    rhs=x2_w[:, cols].bitcast(FP8X4), rhs_scale=x2_scale, start=True, stop=False,
                 )
                 nc.tensor.matmul_mx(
                     out=acc[:], lhsT=w2[:, rows].bitcast(FP8X4), lhsT_scale=w23s[:, rows],
                     rhs=z_w[:].bitcast(FP8X4), rhs_scale=z_s[:], start=False, stop=True,
                 )
-                if c == len(CHUNKS) - 1 and t % 2 == 1:
+                if c == LAST and t % 2 == 1:
                     nc.vector.tensor_copy(h[t][:, cols], acc[:])
                 else:
                     nc.scalar.activation(h[t][:, cols], acc[:], ACT.Copy)
 
         out_rows = out_0.rearrange("(p t) j -> p t j", t=PACK)
         out_words = out_1[0].rearrange("p n t -> p (n t)").bitcast(I32)
-        o_s = sbuf([P, S], U8, "o_s")
+        res_s = sbuf([P, S], U8, "res_s")
         for c, (first, width) in enumerate(CHUNKS):
             cols = slice(first, first + width)
             g4 = sbuf([P, PACK, width], F32, "g4_%d" % c)
             g5 = sbuf([P, PACK, width], F32, "g5_%d" % c)
             m4 = sbuf([P, PACK, width], F32, "m4_%d" % c)
-            o = sbuf([P, PACK, width], F32, "o_%d" % c)
+            res = sbuf([P, PACK, width], F32, "res%d" % c)
             for t in range(PACK):
-                look_up(t < VECTOR_TILES_H[c], g4[:, t, :], h[t], n4_sb, first, width)
+                look_up(t < N4_ON_VECTOR[c], g4[:, t, :], h[t], n4_sb, first, width)
                 look_up(False, g5[:, t, :], h[t], n5_sb, first, width)
             for t in range(PACK):
                 nc.vector.tensor_tensor(m4[:, t, :], h[t][:, cols], g4[:, t, :], ALU.max)
             for t in range(PACK):
-                nc.vector.tensor_tensor(o[:, t, :], m4[:, t, :], g5[:, t, :], ALU.min)
-            nc.sync.dma_start(out_rows[:, :, cols], o[:])
+                nc.vector.tensor_tensor(res[:, t, :], m4[:, t, :], g5[:, t, :], ALU.min)
+            nc.sync.dma_start(out_rows[:, :, cols], res[:])
             rounded = sbuf([P, width, PACK], BF16, "rounded%d" % c)
-            o_w = sbuf([P, width], U32, "o_w%d" % c)
+            res_w = sbuf([P, width], U32, "res_w%d" % c)
             for part in pieces(c):
-                nc.vector.tensor_copy(
-                    rounded[:, part, :].rearrange("p (c i) t -> p c t i", i=4),
-                    o[:, :, part].rearrange("p t (c i) -> p c t i", i=4),
-                )
+                nc.vector.tensor_copy(side_by_side(rounded[:, part, :]), by_tile(res[:, :, part]))
             for part in pieces(c):
                 nc.vector.quantize_mx(
-                    out=o_w[:, part].bitcast(FP8X4), scales=o_s[:, first + part.start : first + part.stop],
+                    out=res_w[:, part].bitcast(FP8X4),
+                    scales=res_s[:, first + part.start : first + part.stop],
                     in_=rounded[:, part, :].rearrange("p j t -> p (j t)"),
                 )
-            nc.sync.dma_start(out_words[:, cols], o_w[:].bitcast(I32))
+            nc.sync.dma_start(out_words[:, cols], res_w[:].bitcast(I32))
+
         for q in range(QUADS):
             queue = nc.sync if q % 2 == 0 else nc.scalar
-            queue.dma_start(out_2[0, 4 * q : 4 * q + 4, :].bitcast(I32), o_s[32 * q : 32 * q + 4, :].bitcast(I32))
+            queue.dma_start(
+                out_2[0, ROWS * q : ROWS * (q + 1), :].bitcast(I32),
+                res_s[32 * q : 32 * q + ROWS, :].bitcast(I32),
+            )

from contextlib import ExitStack

import concourse.mybir as mybir

K, T, S, N, H = 512, 2048, 512, 512, 512
FLOPS = 2 * S * (K * H + H * N + K * N)

F32 = mybir.dt.float32
BF16 = mybir.dt.bfloat16
I32 = mybir.dt.int32
U32 = mybir.dt.uint32
U16 = mybir.dt.uint16
U8 = mybir.dt.uint8
FP8X4 = mybir.dt.float8_e4m3fn_x4
ALU = mybir.AluOpType
ACT = mybir.ActivationFunctionType

P = 128
PACK = 4
QUADS = 4
ROWS = 4
GROUP = 16
NEAR = 4
HALF = S // 2

CHUNKS = ((0, 256), (256, 128), (384, 128))
LAST = len(CHUNKS) - 1
N4_ON_VECTOR = (4, 1, 0)


def tile_picked_mixinmixminmx_none_po_kernel(
    tc, x_words, x_scales, w1_words, w1_scales, gn, w2_words, w2_scales, w3_words, w3_scales,
    offs, n1, n2, n3, two, n4, n5, out_0, out_1, out_2,
):
    nc = tc.nc

    with ExitStack() as ctx:
        keep = ctx.enter_context(tc.tile_pool(name="keep", bufs=1))
        psum = ctx.enter_context(tc.psum_pool(name="psum", bufs=1))

        def sbuf(shape, dtype, name, tag=None):
            return keep.tile(shape, dtype, name=name, tag=tag or name, align_bytes=64)

        def load_list(src, name):
            dst = keep.tile([P, S // GROUP], U16, name=name)
            nc.sync.dma_start(dst[:], src)
            return dst

        def load_words(src, width, name):
            dst = sbuf([P, width], U32, name)
            nc.sync.dma_start(dst[:].bitcast(I32), src[0].rearrange("p n t -> p (n t)").bitcast(I32))
            return dst

        def load_scale_rows(queues, dst, first_row, src):
            for q, queue in enumerate(queues):
                row = 32 * q + first_row
                queue.dma_start(
                    dst[row : row + ROWS, :].bitcast(I32),
                    src[0, ROWS * q : ROWS * (q + 1), :].bitcast(I32),
                )

        def deal_words(engine, src, name):
            dst = sbuf([P, H], U32, name)
            engine.tensor_copy(
                dst[:].bitcast(I32).rearrange("p (t c i) -> p c t i", t=PACK, i=NEAR),
                src[:].bitcast(I32).rearrange("p (c i t) -> p c t i", t=PACK, i=NEAR),
            )
            return dst

        def deal_scales(src, name):
            dst = sbuf([P, H], U8, name)
            nc.gpsimd.tensor_copy(
                dst[:].rearrange("p (t m) -> p t m", t=PACK),
                src[:].rearrange("p (m t) -> p t m", t=PACK),
            )
            return dst

        def pieces(c):
            width = CHUNKS[c][1]
            step = width // 2 if c == LAST else width
            return [slice(a, a + step) for a in range(0, width, step)]

        def entries(lst, first, count):
            return lst[:, first // GROUP : (first + count) // GROUP]

        def look_up(on_vector, dst, window, lst, first, count):
            picked = window[:].indirect(entries(lst, first, count))
            if on_vector:
                nc.vector.tensor_copy(dst, picked)
            else:
                nc.scalar.activation(dst, picked, ACT.Copy)

        def by_tile(planes):
            return planes.rearrange("p t (c i) -> p c t i", i=NEAR)

        def side_by_side(grouped):
            return grouped.rearrange("p (c i) t -> p c t i", i=NEAR)

        x_s = sbuf([P, T], U8, "x_s")
        w1s_raw = sbuf([P, H], U8, "w1s_raw")
        w23s_raw = sbuf([P, H], U8, "w23s_raw")
        nc.vector.memset(x_s[:, : T // 2].bitcast(I32), 0)
        nc.gpsimd.memset(x_s[:, T // 2 :].bitcast(I32), 0)
        nc.vector.memset(w1s_raw[:].bitcast(I32), 0)
        nc.gpsimd.memset(w23s_raw[:].bitcast(I32), 0)

        offs_sb = load_list(offs, "offs_sb")
        two_sb = load_list(two, "two_sb")
        gain = sbuf([P, PACK], F32, "gain")
        nc.scalar.dma_start(gain[:], gn.rearrange("(p t) o -> p (t o)", t=PACK))
        load_scale_rows([nc.sync, nc.sync, nc.scalar, nc.scalar], x_s, 0, x_scales)
        x_w = load_words(x_words, T, "x_w")
        load_scale_rows([nc.sync] * QUADS, w1s_raw, 0, w1_scales)
        w1_raw = load_words(w1_words, H, "w1_raw")
        n1_sb = load_list(n1, "n1_sb")
        n2_sb = load_list(n2, "n2_sb")
        n3_sb = load_list(n3, "n3_sb")
        w3_raw = load_words(w3_words, N, "w3_raw")
        w2_raw = load_words(w2_words, N, "w2_raw")
        load_scale_rows([nc.sync] * QUADS, w23s_raw, 0, w2_scales)
        load_scale_rows([nc.sync] * QUADS, w23s_raw, ROWS, w3_scales)
        n4_sb = load_list(n4, "n4_sb")
        n5_sb = load_list(n5, "n5_sb")

        size = sbuf([P, PACK], F32, "size")
        nc.scalar.activation(size[:], gain[:], ACT.Abs)
        sign = sbuf([P, PACK], BF16, "sign")
        nc.scalar.activation(sign[:], gain[:], ACT.Sign)

        xq_s = sbuf([P, S], U8, "xq_s")
        nc.vector.tensor_copy(xq_s[:], x_s[:].indirect(offs_sb[:]))
        x2_s = [sbuf([P, HALF], U8, "x2_s0")]
        nc.vector.tensor_copy(x2_s[0][:], x_s[:].indirect(entries(two_sb, 0, HALF)))

        xq_w = [sbuf([P, HALF], U32, "xq_w%d" % u) for u in range(2)]
        for u in range(2):
            nc.vector.tensor_copy(xq_w[u][:], x_w[:].indirect(entries(offs_sb, HALF * u, HALF)))
        w1 = deal_words(nc.vector, w1_raw, "w1")
        w1s = deal_scales(w1s_raw, "w1s")

        y = [sbuf([P, S], F32, "y%d" % t) for t in range(PACK)]
        for t in range(PACK):
            rows = slice(P * t, P * (t + 1))
            for u in range(2):
                cols = slice(HALF * u, HALF * (u + 1))
                acc = psum.tile([P, HALF], F32, name="acc", tag="bank%d_%d" % (t, u))
                nc.tensor.matmul_mx(
                    out=acc[:], lhsT=w1[:, rows].bitcast(FP8X4), lhsT_scale=w1s[:, rows],
                    rhs=xq_w[u][:].bitcast(FP8X4), rhs_scale=xq_s[:, cols], start=True, stop=True,
                )
                nc.scalar.activation(y[t][:, cols], acc[:], ACT.Copy, scale=size[:, t : t + 1])

        x2_s.append(sbuf([P, HALF], U8, "x2_s1", tag="w1s_raw"))
        nc.vector.tensor_copy(x2_s[1][:], x_s[:].indirect(entries(two_sb, HALF, HALF)))
        x2_w = sbuf([P, S], U32, "x2_w", tag="w1_raw")
        nc.vector.tensor_copy(x2_w[:], x_w[:].indirect(two_sb[:]))
        w3 = deal_words(nc.gpsimd, w3_raw, "w3")
        w2 = deal_words(nc.gpsimd, w2_raw, "w2")
        w23s = deal_scales(w23s_raw, "w23s")

        z_mx = []
        for c, (first, width) in enumerate(CHUNKS):
            cols = slice(first, first + width)
            g1 = sbuf([P, PACK, width], F32, "g1_%d" % c)
            g2 = sbuf([P, PACK, width], F32, "g2_%d" % c)
            g3 = sbuf([P, PACK, width], F32, "g3_%d" % c)
            m1 = sbuf([P, PACK, width], F32, "m1_%d" % c)
            m2 = sbuf([P, PACK, width], F32, "m2_%d" % c)
            for t in range(PACK):
                look_up(True, g1[:, t, :], y[t], n1_sb, first, width)
                look_up(False, g2[:, t, :], y[t], n2_sb, first, width)
                look_up(False, g3[:, t, :], y[t], n3_sb, first, width)
            for t in range(PACK):
                nc.vector.tensor_tensor(m1[:, t, :], y[t][:, cols], g1[:, t, :], ALU.max)
                nc.vector.tensor_tensor(m2[:, t, :], g2[:, t, :], g3[:, t, :], ALU.max)
            unsigned = sbuf([P, width, PACK], BF16, "unsigned%d" % c)
            z = sbuf([P, width, PACK], BF16, "z%d" % c)
            z_w = sbuf([P, width], U32, "z_w%d" % c)
            z_s = sbuf([P, width], U8, "z_s%d" % c)
            for part in pieces(c):
                nc.vector.tensor_tensor(
                    side_by_side(unsigned[:, part, :]), by_tile(m1[:, :, part]), by_tile(m2[:, :, part]),
                    ALU.subtract,
                )
            for part in pieces(c):
                signs = sign[:].unsqueeze(1).to_broadcast([P, part.stop - part.start, PACK])
                nc.vector.tensor_tensor(z[:, part, :], unsigned[:, part, :], signs, ALU.mult)
            for part in pieces(c):
                nc.vector.quantize_mx(
                    out=z_w[:, part].bitcast(FP8X4), scales=z_s[:, part],
                    in_=z[:, part, :].rearrange("p j t -> p (j t)"),
                )
            z_mx.append((z_w, z_s))

        h = [sbuf([P, S], F32, "h%d" % t) for t in range(PACK)]
        for c, (first, width) in enumerate(CHUNKS):
            cols = slice(first, first + width)
            z_w, z_s = z_mx[c]
            x2_scale = x2_s[first // HALF][:, first % HALF : first % HALF + width]
            for t in range(PACK):
                rows = slice(P * t, P * (t + 1))
                acc = psum.tile([P, width], F32, name="acc", tag="bank%d_%d" % (t, c % 2))
                nc.tensor.matmul_mx(
                    out=acc[:], lhsT=w3[:, rows].bitcast(FP8X4), lhsT_scale=w23s[ROWS:P, rows],
                    rhs=x2_w[:, cols].bitcast(FP8X4), rhs_scale=x2_scale, start=True, stop=False,
                )
                nc.tensor.matmul_mx(
                    out=acc[:], lhsT=w2[:, rows].bitcast(FP8X4), lhsT_scale=w23s[:, rows],
                    rhs=z_w[:].bitcast(FP8X4), rhs_scale=z_s[:], start=False, stop=True,
                )
                if c == LAST and t % 2 == 1:
                    nc.vector.tensor_copy(h[t][:, cols], acc[:])
                else:
                    nc.scalar.activation(h[t][:, cols], acc[:], ACT.Copy)

        out_rows = out_0.rearrange("(p t) j -> p t j", t=PACK)
        out_words = out_1[0].rearrange("p n t -> p (n t)").bitcast(I32)
        res_s = sbuf([P, S], U8, "res_s")
        for c, (first, width) in enumerate(CHUNKS):
            cols = slice(first, first + width)
            g4 = sbuf([P, PACK, width], F32, "g4_%d" % c)
            g5 = sbuf([P, PACK, width], F32, "g5_%d" % c)
            m4 = sbuf([P, PACK, width], F32, "m4_%d" % c)
            res = sbuf([P, PACK, width], F32, "res%d" % c)
            for t in range(PACK):
                look_up(t < N4_ON_VECTOR[c], g4[:, t, :], h[t], n4_sb, first, width)
                look_up(False, g5[:, t, :], h[t], n5_sb, first, width)
            for t in range(PACK):
                nc.vector.tensor_tensor(m4[:, t, :], h[t][:, cols], g4[:, t, :], ALU.max)
            for t in range(PACK):
                nc.vector.tensor_tensor(res[:, t, :], m4[:, t, :], g5[:, t, :], ALU.min)
            nc.sync.dma_start(out_rows[:, :, cols], res[:])
            rounded = sbuf([P, width, PACK], BF16, "rounded%d" % c)
            res_w = sbuf([P, width], U32, "res_w%d" % c)
            for part in pieces(c):
                nc.vector.tensor_copy(side_by_side(rounded[:, part, :]), by_tile(res[:, :, part]))
            for part in pieces(c):
                nc.vector.quantize_mx(
                    out=res_w[:, part].bitcast(FP8X4),
                    scales=res_s[:, first + part.start : first + part.stop],
                    in_=rounded[:, part, :].rearrange("p j t -> p (j t)"),
                )
            nc.sync.dma_start(out_words[:, cols], res_w[:].bitcast(I32))

        for q in range(QUADS):
            queue = nc.sync if q % 2 == 0 else nc.scalar
            queue.dma_start(
                out_2[0, ROWS * q : ROWS * (q + 1), :].bitcast(I32),
                res_s[32 * q : 32 * q + ROWS, :].bitcast(I32),
            )
